import numpy as np
import ml_dtypes


def mxq(x, axis, fmt="e4m3"):
    dtype, down = {"e4m3": (ml_dtypes.float8_e4m3fn, 7), "e5m2": (ml_dtypes.float8_e5m2, 14)}[fmt]
    v = np.moveaxis(np.asarray(x, np.float32).astype(ml_dtypes.bfloat16).astype(np.float64), axis, -1)
    blocks = v.reshape(v.shape[:-1] + (-1, 32))
    amax = np.abs(blocks).max(-1, keepdims=True)
    byte = np.maximum(np.where(amax > 0, np.frexp(amax)[1] - 1 + 127, 0) - down, 1)
    scale = np.exp2(byte - 127.0)
    codes = (blocks / scale).astype(np.float32).astype(dtype).astype(np.float64)
    return np.moveaxis((codes * scale).reshape(v.shape), -1, axis)


WIDE = False


def mx_kscale(k):
    if not WIDE:
        return np.ones(k)
    levels = np.array([10, -10, 5, -5, 0])
    if k % 512:
        return np.exp2(np.random.permutation(np.resize(levels, k // 32))).repeat(32)
    a = np.empty((k // 512, 16))
    for p in range(k // 512):
        a[p, :8] = np.random.permutation(np.resize(levels, 8))
        for g in range(8):
            far = levels[np.abs(levels - a[p, g]) >= 10]
            a[p, g + 8] = far[np.random.randint(len(far))]
    return np.exp2(a.ravel()).repeat(32)


def f64(x):
    return np.asarray(x).astype(np.float64)


def striped(idx):
    return np.tile(np.asarray(idx).reshape(-1, 16).T, (8, 1)).astype(np.uint16)


def unstriped(offs):
    return offs[:16].T.reshape(-1).astype(np.int64)


def striped8(idx):
    return np.asarray(idx).reshape(8, -1, 16).transpose(0, 2, 1).reshape(128, -1).astype(np.uint16)


def unstriped8(offs):
    return offs.reshape(8, 16, -1).transpose(0, 2, 1).reshape(8, -1).astype(np.int64)


def pick8(x, idx, run):
    r = np.arange(len(x))
    return x[r[:, None], idx[r % (8 * run) // run]]


E2M1 = np.array([0.0, 0.5, 1.0, 1.5, 2.0, 3.0, 4.0, 6.0, -0.0, -0.5, -1.0, -1.5, -2.0, -3.0, -4.0, -6.0])


def pack_weight(w, fmt):
    k, n = w.shape
    w = f64(np.asarray(w, np.float32).astype(ml_dtypes.bfloat16)).reshape(k // 32, 32, n)
    amax = np.abs(w).max(1)
    if fmt == "e4m3":
        byte = np.frexp(amax)[1] - 1 + 127 - 7
    else:
        mant, ex = np.frexp(amax / 6.0)
        byte = np.where(mant > 0.5, ex, ex - 1) + 127
    byte = np.clip(np.where(amax > 0, byte, 1), 1, 254)
    scaled = (w * np.exp2(127.0 - byte)[:, None, :]).reshape(k, n).astype(np.float32)
    by_word = np.ascontiguousarray(scaled.reshape(k // 512, 128, 4, n).transpose(0, 1, 3, 2))
    if fmt == "e4m3":
        words = by_word.astype(ml_dtypes.float8_e4m3fn).view(np.uint8)
    else:
        c = by_word.astype(ml_dtypes.float4_e2m1fn).view(np.uint8) & 0xF
        words = (c[..., 0::2] | (c[..., 1::2] << 4)).reshape(k // 512, 128, 2 * n)
    return np.ascontiguousarray(words), np.ascontiguousarray(byte.astype(np.uint8).reshape(k // 512, 16, n))


def unpack_weight(words, scales, fmt):
    g, _, n = scales.shape
    words = np.ascontiguousarray(words).reshape(g, 128, n, -1)
    if fmt == "e4m3":
        vals = words.view(ml_dtypes.float8_e4m3fn).astype(np.float64)
    else:
        nib = np.empty((g, 128, n, 4), np.uint8)
        nib[..., 0::2] = words & 0xF
        nib[..., 1::2] = words >> 4
        vals = E2M1[nib]
    vals = vals * np.repeat(np.exp2(scales.astype(np.float64) - 127.0), 8, axis=1)[..., None]
    return vals.transpose(0, 1, 3, 2).reshape(g * 512, n)


K, J, R, T, F, O, C, N, S = 512, 512, 512, 1024, 1024, 256, 1024, 256, 1024


def setup_inputs():
    n = np.random.standard_normal
    idx = np.stack([np.random.permutation(T)[:J] for _ in range(8)])
    idx2 = np.stack([np.random.permutation(T)[:J] for _ in range(8)])
    idx3 = np.stack([np.random.permutation(F)[:R] for _ in range(8)])
    idx4 = np.stack([np.random.permutation(C)[:J] for _ in range(8)])
    idx5 = np.stack([np.random.permutation(C)[:O] for _ in range(8)])
    idx6 = np.stack([np.random.permutation(C)[:O] for _ in range(8)])
    idx7 = np.random.permutation(S)[:N]
    fk = mx_kscale(K)
    fr = mx_kscale(R)
    vsp = pack_weight(n((R, S)) * 1 / np.sqrt(R) / fr[:, None], "e2m1")
    return {
        "ta": (np.random.randint(-7, 8, (K, T)).astype(np.float64)).astype(np.float32),
        "ga": ((np.random.randint(8, 19, (K, 1)) / 64.0) * fk[:, None]).astype(np.float32),
        "gb": ((np.random.randint(8, 19, (K, 1)) / 64.0) * fk[:, None]).astype(np.float32),
        "ua": (np.random.randint(-7, 8, (K, F)).astype(np.float64)).astype(np.float32),
        "ha": ((np.random.randint(8, 25, (K, 1)) / 1024.0) / fk[:, None]).astype(np.float32),
        "sa": (np.random.uniform(0.5, 1.6, (R, 1)) * fr[:, None]).astype(np.float32),
        "sb": (np.random.uniform(0.5, 1.6, (R, 1)) * fr[:, None]).astype(np.float32),
        "vs_words": vsp[0],
        "vs_scales": vsp[1],
        "offs": striped8(idx),
        "offs2": striped8(idx2),
        "offs3": striped8(idx3),
        "offs4": striped8(idx4),
        "offs5": striped8(idx5),
        "offs6": striped8(idx6),
        "offs7": striped(idx7),
    }


def reference(ta, ga, gb, ua, ha, sa, sb, vs_words, vs_scales, offs, offs2, offs3, offs4, offs5, offs6, offs7):
    idx = unstriped8(offs)
    idx2 = unstriped8(offs2)
    idx3 = unstriped8(offs3)
    idx4 = unstriped8(offs4)
    idx5 = unstriped8(offs5)
    idx6 = unstriped8(offs6)
    idx7 = unstriped(offs7)
    vsu = unpack_weight(vs_words, vs_scales, "e2m1")
    xc = pick8(f64(ta), idx, 64) * f64(ga) - pick8(f64(ta), idx2, 64) * f64(gb)
    wc = pick8(f64(ua), idx3, 64) * f64(ha)
    wcq = mxq(wc, 0, "e4m3")
    xcq = mxq(xc, 0, "e4m3")
    a = wcq.T @ xcq
    pw = np.zeros((R, C))
    pw[np.arange(R)[:, None], idx4[np.arange(R) % 512 // 64]] = a
    hid = np.abs(pick8(pw, idx5, 64) * f64(sa) - pick8(pw, idx6, 64) * f64(sb))
    vsidx7g = vsu[:, idx7]
    hidq = mxq(hid, 0, "e4m3")
    y = vsidx7g.T @ hidq
    return y

@@ -1,0 +1,206 @@
+from contextlib import ExitStack
+
+import concourse.mybir as mybir
+
+F32 = mybir.dt.float32
+BF16 = mybir.dt.bfloat16
+I32 = mybir.dt.int32
+U32 = mybir.dt.uint32
+U16 = mybir.dt.uint16
+U8 = mybir.dt.uint8
+FP8X4 = mybir.dt.float8_e4m3fn_x4
+FP4X4 = mybir.dt.float4_e2m1fn_x4
+ACT = mybir.ActivationFunctionType
+ALU = mybir.AluOpType
+
+K, J, R, T, F, O, C, N, S = 512, 512, 512, 1024, 1024, 256, 1024, 256, 1024
+FLOPS = 2 * K * R * J + 2 * R * N * O
+
+P = 128
+PACK = 4
+STRIPE = 16
+HALF = J // 2
+QUARTER = J // 4
+
+
+def tile_picked_codegap_codes_one_boardpair_store_plain_kernel(
+    tc, ta, ga, gb, ua, ha, sa, sb, vs_words, vs_scales, offs, offs2, offs3, offs4, offs5, offs6, offs7, out
+):
+    nc = tc.nc
+    with ExitStack() as ctx:
+        keep = ctx.enter_context(tc.tile_pool(name="keep", bufs=1))
+        psum_a = ctx.enter_context(tc.psum_pool(name="psum_a", bufs=6))
+        psum_y = ctx.enter_context(tc.psum_pool(name="psum_y", bufs=2))
+
+        def list_tile(name, src):
+            tile = keep.tile(list(src.shape), U16, name=name)
+            nc.sync.dma_start(tile[:], src)
+            return tile
+
+        def steps_tile(name, src):
+            tile = keep.tile([P, PACK], F32, name=name)
+            nc.sync.dma_start(tile[:], src.rearrange("(p t) o -> p (t o)", t=PACK))
+            return tile
+
+        def table_tile(name, src, t):
+            tile = keep.tile([P, src.shape[1]], F32, name=name)
+            nc.sync.dma_start(tile[:], src.rearrange("(p t) c -> t p c", t=PACK)[t])
+            return tile
+
+        idx3 = list_tile("idx3", offs3)
+        ha_t = steps_tile("ha_t", ha)
+        ua_rows = [table_tile(f"ua{t}", ua, t) for t in range(PACK)]
+        idx1 = list_tile("idx1", offs)
+        idx2 = list_tile("idx2", offs2)
+        ga_t = steps_tile("ga_t", ga)
+        gb_t = steps_tile("gb_t", gb)
+        ta_rows = [table_tile(f"ta{t}", ta, t) for t in range(2)]
+        idx7 = list_tile("idx7", offs7)
+        vs_scale_table = keep.tile([P, S], U8, name="vs_scale_table")
+        nc.vector.memset(vs_scale_table[:].bitcast(I32), 0)
+        for q in range(4):
+            nc.sync.dma_start(
+                vs_scale_table[32 * q : 32 * q + 4, :].bitcast(I32), vs_scales[0, 4 * q : 4 * q + 4, :].bitcast(I32)
+            )
+        ta_rows.extend(table_tile(f"ta{t}", ta, t) for t in range(2, PACK))
+        vs_word_table = keep.tile([P, S], U16, name="vs_word_table")
+        nc.sync.dma_start(vs_word_table[:].bitcast(I32), vs_words[0].bitcast(I32))
+        idx4 = list_tile("idx4", offs4)
+        idx5 = list_tile("idx5", offs5)
+        idx6 = list_tile("idx6", offs6)
+
+        sa_t = steps_tile("sa_t", sa)
+        sb_t = steps_tile("sb_t", sb)
+
+        boards = [keep.tile([P, C], F32, name=f"board{t}") for t in range(PACK)]
+        for board in boards:
+            nc.vector.memset(board[:], 0.0)
+
+        def fetch(dst, table, offsets, steps, t):
+            nc.scalar.activation(dst, table[:].indirect(offsets), ACT.Copy, scale=steps[:, t : t + 1])
+
+        wc_planes = keep.tile([P, PACK, R], BF16, name="wc_planes")
+        for t in range(PACK):
+            fetch(wc_planes[:, t, :], ua_rows[t], idx3[:], ha_t, t)
+        wc_words = keep.tile([P, R * PACK], BF16, name="wc_words", align_bytes=64)
+        nc.vector.tensor_copy(
+            wc_words[:].rearrange("p (u m t) -> p u m t", u=PACK, t=PACK),
+            wc_planes[:].rearrange("p t (m u) -> p u m t", u=PACK),
+        )
+        wc_codes = keep.tile([P, R], U32, name="wc_codes", align_bytes=64)
+        wc_scales = keep.tile([P, R], U8, name="wc_scales", align_bytes=64)
+        nc.vector.quantize_mx(wc_codes[:].bitcast(FP8X4), wc_scales[:], wc_words[:])
+
+        vs_scale_picked = keep.tile([P, N], U8, name="vs_scale_picked", align_bytes=64)
+        nc.vector.tensor_copy(vs_scale_picked[:], vs_scale_table[:].indirect(idx7[:]))
+        vs_word_picked = keep.tile([P, N], U16, name="vs_word_picked", align_bytes=64)
+        nc.vector.tensor_copy(vs_word_picked[:], vs_word_table[:].indirect(idx7[:]))
+
+        def half_cols(h):
+            return slice(h * HALF // STRIPE, (h + 1) * HALF // STRIPE)
+
+        def product(u, codes, scales, slots):
+            acc = psum_a.tile([P, slots.stop - slots.start], F32, name="acc")
+            cols = slice(u * P, (u + 1) * P)
+            nc.tensor.matmul_mx(
+                acc[:], lhsT=wc_codes[:, cols].bitcast(FP8X4), lhsT_scale=wc_scales[:, cols],
+                rhs=codes[:, slots].bitcast(FP8X4), rhs_scale=scales[:, slots], start=True, stop=True,
+            )
+            return acc
+
+        def put(u, h, staged):
+            nc.vector.tensor_copy(boards[u][:].indirect(idx4[:, half_cols(h)]), staged)
+
+        def quantised(name, words, width):
+            codes = keep.tile([P, width], U32, name=name + "_codes", align_bytes=64)
+            scales = keep.tile([P, width], U8, name=name + "_scales", align_bytes=64)
+            nc.vector.quantize_mx(codes[:].bitcast(FP8X4), scales[:], words[:].rearrange("p c t -> p (c t)"))
+            return codes, scales
+
+        terms0 = keep.tile([P, 2, PACK - 1, HALF], F32, name="terms0")
+        terms1 = keep.tile([P, 2 * PACK * HALF], F32, name="terms1")
+
+        def term1(side, t):
+            start = (side * PACK + t) * HALF
+            return terms1[:, start : start + HALF]
+
+        xc0 = [keep.tile([P, QUARTER, PACK], BF16, name=f"xc0_{q}", align_bytes=64) for q in range(2)]
+        for t in range(PACK):
+            pair = [terms0[:, side, t, :] if t < PACK - 1 else term1(side, 0) for side in range(2)]
+            fetch(pair[0], ta_rows[t], idx1[:, half_cols(0)], ga_t, t)
+            fetch(pair[1], ta_rows[t], idx2[:, half_cols(0)], gb_t, t)
+            for q in range(2):
+                cols = slice(q * QUARTER, (q + 1) * QUARTER)
+                nc.vector.tensor_tensor(xc0[q][:, :, t], pair[0][:, cols], pair[1][:, cols], ALU.subtract)
+        x0_codes = keep.tile([P, HALF], U32, name="x0_codes", align_bytes=64)
+        x0_scales = keep.tile([P, HALF], U8, name="x0_scales", align_bytes=64)
+        for q in range(2):
+            cols = slice(q * QUARTER, (q + 1) * QUARTER)
+            nc.vector.quantize_mx(
+                x0_codes[:, cols].bitcast(FP8X4), x0_scales[:, cols], xc0[q][:].rearrange("p c t -> p (c t)")
+            )
+        lead = [product(0, x0_codes, x0_scales, slice(q * QUARTER, (q + 1) * QUARTER)) for q in range(2)]
+        acc0 = [product(u, x0_codes, x0_scales, slice(0, HALF)) for u in range(1, PACK)]
+        for q in range(2):
+            start = (q * PACK + 2) * HALF - QUARTER // 2
+            staged = terms1[:, start : start + QUARTER]
+            nc.vector.tensor_copy(staged, lead[q][:])
+            nc.vector.tensor_copy(
+                boards[0][:].indirect(idx4[:, q * QUARTER // STRIPE : (q + 1) * QUARTER // STRIPE]), staged
+            )
+        for u in range(1, PACK - 1):
+            staged = keep.tile([P, HALF], F32, name=f"staged0_{u}")
+            nc.scalar.copy(staged[:], acc0[u - 1][:])
+            put(u, 0, staged[:])
+
+        for side, t in ((0, 3), (1, 3), (0, 0), (1, 0), (0, 1), (0, 2), (1, 1), (1, 2)):
+            fetch(term1(side, t), ta_rows[t], (idx1, idx2)[side][:, half_cols(1)], (ga_t, gb_t)[side], t)
+        xc1 = keep.tile([P, HALF, PACK], BF16, name="xc1", align_bytes=64)
+        sides = terms1[:].rearrange("p (s t c i) -> p s c t i", s=2, t=PACK, i=4)
+        nc.vector.tensor_tensor(xc1[:].rearrange("p (c i) t -> p c t i", i=4), sides[:, 0], sides[:, 1], ALU.subtract)
+        x1_codes, x1_scales = quantised("xc1", xc1, HALF)
+        staged_last = term1(0, 0)
+        nc.scalar.copy(staged_last, acc0[PACK - 2][:])
+        put(PACK - 1, 0, staged_last)
+
+        first = keep.tile([P, PACK, O], F32, name="first")
+        second = keep.tile([P, PACK, O], F32, name="second")
+        staged1 = [keep.tile([P, HALF], F32, name=f"staged1_{u}") for u in range(PACK)]
+        for u in range(PACK):
+            nc.scalar.copy(staged1[u][:], product(u, x1_codes, x1_scales, slice(0, HALF))[:])
+        for u in range(PACK):
+            put(u, 1, staged1[u][:])
+        for u in range(PACK):
+            fetch(first[:, u, :], boards[u], idx5[:], sa_t, u)
+            fetch(second[:, u, :], boards[u], idx6[:], sb_t, u)
+
+        gap = keep.tile([P, PACK, O], BF16, name="gap")
+        nc.vector.tensor_tensor(gap[:, : PACK - 1, :], first[:, : PACK - 1, :], second[:, : PACK - 1, :], ALU.subtract)
+        nc.vector.tensor_tensor(gap[:, PACK - 1, :], first[:, PACK - 1, :], second[:, PACK - 1, :], ALU.subtract)
+        hid_lo = keep.tile([P, O // 2, PACK], BF16, name="hid_lo", align_bytes=64)
+        hid_hi = keep.tile([P, O // 2, PACK], BF16, name="hid_hi", align_bytes=64)
+        nc.scalar.activation(
+            hid_hi[:].rearrange("p (c i) t -> p c t i", i=4),
+            gap[:, :, O // 2 :].rearrange("p t (c i) -> p c t i", i=4),
+            ACT.Abs,
+        )
+        gap_lo = gap[:, :, : O // 2].rearrange("p t c -> p c t")
+        nc.vector.scalar_tensor_tensor(hid_lo[:], gap_lo, -1.0, gap_lo, ALU.mult, ALU.max)
+        hid_codes = keep.tile([P, O], U32, name="hid_codes", align_bytes=64)
+        hid_scales = keep.tile([P, O], U8, name="hid_scales", align_bytes=64)
+        for part, words in enumerate((hid_lo, hid_hi)):
+            cols = slice(part * O // 2, (part + 1) * O // 2)
+            nc.vector.quantize_mx(
+                hid_codes[:, cols].bitcast(FP8X4), hid_scales[:, cols], words[:].rearrange("p c t -> p (c t)")
+            )
+
+        for b, (engine_copy, queue) in enumerate(((nc.vector.tensor_copy, nc.sync), (nc.scalar.copy, nc.scalar))):
+            rows = slice(b * P, (b + 1) * P)
+            y = psum_y.tile([P, O], F32, name="y")
+            nc.tensor.matmul_mx(
+                y[:], lhsT=vs_word_picked[:, rows].bitcast(FP4X4), lhsT_scale=vs_scale_picked[:, rows],
+                rhs=hid_codes[:].bitcast(FP8X4), rhs_scale=hid_scales[:], start=True, stop=True,
+            )
+            result = keep.tile([P, O], F32, name=f"result{b}")
+            engine_copy(result[:], y[:])
+            queue.dma_start(out[rows, :], result[:])

@@ -47,6 +47,10 @@ def tile_picked_codegap_codes_one_boardpair_store_plain_kernel(
             nc.sync.dma_start(tile[:], src.rearrange("(p t) c -> t p c", t=PACK)[t])
             return tile
 
+        warm_in = keep.tile([P, 1], F32, name="warm_in")
+        warm_out = keep.tile([P, 1], F32, name="warm_out")
+        nc.vector.memset(warm_in[:], 0.0)
+        nc.scalar.activation(warm_out[:], warm_in[:], ACT.Copy)
         idx3 = list_tile("idx3", offs3)
         ha_t = steps_tile("ha_t", ha)
         ua_rows = [table_tile(f"ua{t}", ua, t) for t in range(PACK)]

@@ -21,6 +21,8 @@ PACK = 4
 STRIPE = 16
 HALF = J // 2
 QUARTER = J // 4
+PART = O // 2
+SLOTS = PACK + 1
 
 
 def tile_picked_codegap_codes_one_boardpair_store_plain_kernel(
@@ -29,8 +31,7 @@ def tile_picked_codegap_codes_one_boardpair_store_plain_kernel(
     nc = tc.nc
     with ExitStack() as ctx:
         keep = ctx.enter_context(tc.tile_pool(name="keep", bufs=1))
-        psum_a = ctx.enter_context(tc.psum_pool(name="psum_a", bufs=6))
-        psum_y = ctx.enter_context(tc.psum_pool(name="psum_y", bufs=2))
+        psum = ctx.enter_context(tc.psum_pool(name="psum", bufs=8))
 
         def list_tile(name, src):
             tile = keep.tile(list(src.shape), U16, name=name)
@@ -51,9 +52,10 @@ def tile_picked_codegap_codes_one_boardpair_store_plain_kernel(
         warm_out = keep.tile([P, 1], F32, name="warm_out")
         nc.vector.memset(warm_in[:], 0.0)
         nc.scalar.activation(warm_out[:], warm_in[:], ACT.Copy)
+        ua_rows = [table_tile("ua0", ua, 0)]
         idx3 = list_tile("idx3", offs3)
         ha_t = steps_tile("ha_t", ha)
-        ua_rows = [table_tile(f"ua{t}", ua, t) for t in range(PACK)]
+        ua_rows.extend(table_tile(f"ua{t}", ua, t) for t in range(1, PACK))
         idx1 = list_tile("idx1", offs)
         idx2 = list_tile("idx2", offs2)
         ga_t = steps_tile("ga_t", ga)
@@ -88,8 +90,8 @@ def tile_picked_codegap_codes_one_boardpair_store_plain_kernel(
             fetch(wc_planes[:, t, :], ua_rows[t], idx3[:], ha_t, t)
         wc_words = keep.tile([P, R * PACK], BF16, name="wc_words", align_bytes=64)
         nc.vector.tensor_copy(
-            wc_words[:].rearrange("p (u m t) -> p u m t", u=PACK, t=PACK),
-            wc_planes[:].rearrange("p t (m u) -> p u m t", u=PACK),
+            wc_words[:].rearrange("p (u m i t) -> p m t i u", u=PACK, i=2, t=PACK),
+            wc_planes[:].rearrange("p t (m i u) -> p m t i u", i=2, u=PACK),
         )
         wc_codes = keep.tile([P, R], U32, name="wc_codes", align_bytes=64)
         wc_scales = keep.tile([P, R], U8, name="wc_scales", align_bytes=64)
@@ -104,7 +106,7 @@ def tile_picked_codegap_codes_one_boardpair_store_plain_kernel(
             return slice(h * HALF // STRIPE, (h + 1) * HALF // STRIPE)
 
         def product(u, codes, scales, slots):
-            acc = psum_a.tile([P, slots.stop - slots.start], F32, name="acc")
+            acc = psum.tile([P, slots.stop - slots.start], F32, name="acc")
             cols = slice(u * P, (u + 1) * P)
             nc.tensor.matmul_mx(
                 acc[:], lhsT=wc_codes[:, cols].bitcast(FP8X4), lhsT_scale=wc_scales[:, cols],
@@ -121,21 +123,29 @@ def tile_picked_codegap_codes_one_boardpair_store_plain_kernel(
             nc.vector.quantize_mx(codes[:].bitcast(FP8X4), scales[:], words[:].rearrange("p c t -> p (c t)"))
             return codes, scales
 
-        terms0 = keep.tile([P, 2, PACK - 1, HALF], F32, name="terms0")
-        terms1 = keep.tile([P, 2 * PACK * HALF], F32, name="terms1")
+        terms = keep.tile([P, 2 * SLOTS * HALF], F32, name="terms")
 
-        def term1(side, t):
-            start = (side * PACK + t) * HALF
-            return terms1[:, start : start + HALF]
+        def term(side, h, t):
+            start = (2 * (h + t) + side) * HALF
+            return terms[:, start : start + HALF]
+
+        def planes(side, h, ts, cols):
+            slots = terms[:].rearrange("p (n s c) -> p s n c", s=2, n=SLOTS)
+            return slots[:, side, h + ts.start : h + ts.stop, cols].rearrange("p t (c i) -> p c t i", i=4)
+
+        def subtract(words, h, ts, cols):
+            nc.vector.tensor_tensor(
+                words[:, :, ts].rearrange("p (c i) t -> p c t i", i=4),
+                planes(0, h, ts, cols), planes(1, h, ts, cols), ALU.subtract,
+            )
 
         xc0 = [keep.tile([P, QUARTER, PACK], BF16, name=f"xc0_{q}", align_bytes=64) for q in range(2)]
         for t in range(PACK):
-            pair = [terms0[:, side, t, :] if t < PACK - 1 else term1(side, 0) for side in range(2)]
-            fetch(pair[0], ta_rows[t], idx1[:, half_cols(0)], ga_t, t)
-            fetch(pair[1], ta_rows[t], idx2[:, half_cols(0)], gb_t, t)
-            for q in range(2):
-                cols = slice(q * QUARTER, (q + 1) * QUARTER)
-                nc.vector.tensor_tensor(xc0[q][:, :, t], pair[0][:, cols], pair[1][:, cols], ALU.subtract)
+            fetch(term(0, 0, t), ta_rows[t], idx1[:, half_cols(0)], ga_t, t)
+            fetch(term(1, 0, t), ta_rows[t], idx2[:, half_cols(0)], gb_t, t)
+            if t % 2 == 1:
+                for q in range(2):
+                    subtract(xc0[q], 0, slice(t - 1, t + 1), slice(q * QUARTER, (q + 1) * QUARTER))
         x0_codes = keep.tile([P, HALF], U32, name="x0_codes", align_bytes=64)
         x0_scales = keep.tile([P, HALF], U8, name="x0_scales", align_bytes=64)
         for q in range(2):
@@ -146,8 +156,8 @@ def tile_picked_codegap_codes_one_boardpair_store_plain_kernel(
         lead = [product(0, x0_codes, x0_scales, slice(q * QUARTER, (q + 1) * QUARTER)) for q in range(2)]
         acc0 = [product(u, x0_codes, x0_scales, slice(0, HALF)) for u in range(1, PACK)]
         for q in range(2):
-            start = (q * PACK + 2) * HALF - QUARTER // 2
-            staged = terms1[:, start : start + QUARTER]
+            start = (2 * (1 + q) + 1) * HALF - QUARTER // 2
+            staged = terms[:, start : start + QUARTER]
             nc.vector.tensor_copy(staged, lead[q][:])
             nc.vector.tensor_copy(
                 boards[0][:].indirect(idx4[:, q * QUARTER // STRIPE : (q + 1) * QUARTER // STRIPE]), staged
@@ -157,13 +167,13 @@ def tile_picked_codegap_codes_one_boardpair_store_plain_kernel(
             nc.scalar.copy(staged[:], acc0[u - 1][:])
             put(u, 0, staged[:])
 
-        for side, t in ((0, 3), (1, 3), (0, 0), (1, 0), (0, 1), (0, 2), (1, 1), (1, 2)):
-            fetch(term1(side, t), ta_rows[t], (idx1, idx2)[side][:, half_cols(1)], (ga_t, gb_t)[side], t)
+        for t in (3, 2, 0, 1):
+            fetch(term(0, 1, t), ta_rows[t], idx1[:, half_cols(1)], ga_t, t)
+            fetch(term(1, 1, t), ta_rows[t], idx2[:, half_cols(1)], gb_t, t)
         xc1 = keep.tile([P, HALF, PACK], BF16, name="xc1", align_bytes=64)
-        sides = terms1[:].rearrange("p (s t c i) -> p s c t i", s=2, t=PACK, i=4)
-        nc.vector.tensor_tensor(xc1[:].rearrange("p (c i) t -> p c t i", i=4), sides[:, 0], sides[:, 1], ALU.subtract)
+        subtract(xc1, 1, slice(0, PACK), slice(0, HALF))
         x1_codes, x1_scales = quantised("xc1", xc1, HALF)
-        staged_last = term1(0, 0)
+        staged_last = term(1, 1, 1)
         nc.scalar.copy(staged_last, acc0[PACK - 2][:])
         put(PACK - 1, 0, staged_last)
 
@@ -181,30 +191,24 @@ def tile_picked_codegap_codes_one_boardpair_store_plain_kernel(
         gap = keep.tile([P, PACK, O], BF16, name="gap")
         nc.vector.tensor_tensor(gap[:, : PACK - 1, :], first[:, : PACK - 1, :], second[:, : PACK - 1, :], ALU.subtract)
         nc.vector.tensor_tensor(gap[:, PACK - 1, :], first[:, PACK - 1, :], second[:, PACK - 1, :], ALU.subtract)
-        hid_lo = keep.tile([P, O // 2, PACK], BF16, name="hid_lo", align_bytes=64)
-        hid_hi = keep.tile([P, O // 2, PACK], BF16, name="hid_hi", align_bytes=64)
+        hid_words = [keep.tile([P, PART, PACK], BF16, name=f"hid_words{part}", align_bytes=64) for part in range(2)]
         nc.scalar.activation(
-            hid_hi[:].rearrange("p (c i) t -> p c t i", i=4),
-            gap[:, :, O // 2 :].rearrange("p t (c i) -> p c t i", i=4),
+            hid_words[0][:].rearrange("p (c i) t -> p c t i", i=4),
+            gap[:, :, :PART].rearrange("p t (c i) -> p c t i", i=4),
             ACT.Abs,
         )
-        gap_lo = gap[:, :, : O // 2].rearrange("p t c -> p c t")
-        nc.vector.scalar_tensor_tensor(hid_lo[:], gap_lo, -1.0, gap_lo, ALU.mult, ALU.max)
-        hid_codes = keep.tile([P, O], U32, name="hid_codes", align_bytes=64)
-        hid_scales = keep.tile([P, O], U8, name="hid_scales", align_bytes=64)
-        for part, words in enumerate((hid_lo, hid_hi)):
-            cols = slice(part * O // 2, (part + 1) * O // 2)
-            nc.vector.quantize_mx(
-                hid_codes[:, cols].bitcast(FP8X4), hid_scales[:, cols], words[:].rearrange("p c t -> p (c t)")
-            )
-
-        for b, (engine_copy, queue) in enumerate(((nc.vector.tensor_copy, nc.sync), (nc.scalar.copy, nc.scalar))):
-            rows = slice(b * P, (b + 1) * P)
-            y = psum_y.tile([P, O], F32, name="y")
-            nc.tensor.matmul_mx(
-                y[:], lhsT=vs_word_picked[:, rows].bitcast(FP4X4), lhsT_scale=vs_scale_picked[:, rows],
-                rhs=hid_codes[:].bitcast(FP8X4), rhs_scale=hid_scales[:], start=True, stop=True,
-            )
-            result = keep.tile([P, O], F32, name=f"result{b}")
-            engine_copy(result[:], y[:])
-            queue.dma_start(out[rows, :], result[:])
+        gap_rest = gap[:, :, PART:].rearrange("p t c -> p c t")
+        nc.vector.scalar_tensor_tensor(hid_words[1][:], gap_rest, -1.0, gap_rest, ALU.mult, ALU.max)
+        results = [keep.tile([P, O], F32, name=f"result{b}") for b in range(2)]
+        for part in range(2):
+            codes, scales = quantised(f"hid{part}", hid_words[part], PART)
+            for b, engine_copy in enumerate((nc.vector.tensor_copy, nc.scalar.copy)):
+                rows = slice(b * P, (b + 1) * P)
+                y = psum.tile([P, PART], F32, name="acc")
+                nc.tensor.matmul_mx(
+                    y[:], lhsT=vs_word_picked[:, rows].bitcast(FP4X4), lhsT_scale=vs_scale_picked[:, rows],
+                    rhs=codes[:].bitcast(FP8X4), rhs_scale=scales[:], start=True, stop=True,
+                )
+                engine_copy(results[b][:, part * PART : (part + 1) * PART], y[:])
+        for b, queue in enumerate((nc.sync, nc.scalar)):
+            queue.dma_start(out[b * P : (b + 1) * P, :], results[b][:])

@@ -133,8 +133,8 @@ def tile_picked_codegap_codes_one_boardpair_store_plain_kernel(
             slots = terms[:].rearrange("p (n s c) -> p s n c", s=2, n=SLOTS)
             return slots[:, side, h + ts.start : h + ts.stop, cols].rearrange("p t (c i) -> p c t i", i=4)
 
-        def subtract(words, h, ts, cols):
-            nc.vector.tensor_tensor(
+        def subtract(engine, words, h, ts, cols):
+            engine.tensor_tensor(
                 words[:, :, ts].rearrange("p (c i) t -> p c t i", i=4),
                 planes(0, h, ts, cols), planes(1, h, ts, cols), ALU.subtract,
             )
@@ -145,7 +145,7 @@ def tile_picked_codegap_codes_one_boardpair_store_plain_kernel(
             fetch(term(1, 0, t), ta_rows[t], idx2[:, half_cols(0)], gb_t, t)
             if t % 2 == 1:
                 for q in range(2):
-                    subtract(xc0[q], 0, slice(t - 1, t + 1), slice(q * QUARTER, (q + 1) * QUARTER))
+                    subtract(nc.vector, xc0[q], 0, slice(t - 1, t + 1), slice(q * QUARTER, (q + 1) * QUARTER))
         x0_codes = keep.tile([P, HALF], U32, name="x0_codes", align_bytes=64)
         x0_scales = keep.tile([P, HALF], U8, name="x0_scales", align_bytes=64)
         for q in range(2):
@@ -171,7 +171,8 @@ def tile_picked_codegap_codes_one_boardpair_store_plain_kernel(
             fetch(term(0, 1, t), ta_rows[t], idx1[:, half_cols(1)], ga_t, t)
             fetch(term(1, 1, t), ta_rows[t], idx2[:, half_cols(1)], gb_t, t)
         xc1 = keep.tile([P, HALF, PACK], BF16, name="xc1", align_bytes=64)
-        subtract(xc1, 1, slice(0, PACK), slice(0, HALF))
+        for ts in (slice(2, 4), slice(0, 1), slice(1, 2)):
+            subtract(nc.gpsimd, xc1, 1, ts, slice(0, HALF))
         x1_codes, x1_scales = quantised("xc1", xc1, HALF)
         staged_last = term(1, 1, 1)
         nc.scalar.copy(staged_last, acc0[PACK - 2][:])

from contextlib import ExitStack

import concourse.mybir as mybir

F32 = mybir.dt.float32
BF16 = mybir.dt.bfloat16
I32 = mybir.dt.int32
U32 = mybir.dt.uint32
U16 = mybir.dt.uint16
U8 = mybir.dt.uint8
FP8X4 = mybir.dt.float8_e4m3fn_x4
FP4X4 = mybir.dt.float4_e2m1fn_x4
ACT = mybir.ActivationFunctionType
ALU = mybir.AluOpType

K, J, R, T, F, O, C, N, S = 512, 512, 512, 1024, 1024, 256, 1024, 256, 1024
FLOPS = 2 * K * R * J + 2 * R * N * O

P = 128
PACK = 4
STRIPE = 16
HALF = J // 2
QUARTER = J // 4
PART = O // 2
SLOTS = PACK + 1


def tile_picked_codegap_codes_one_boardpair_store_plain_kernel(
    tc, ta, ga, gb, ua, ha, sa, sb, vs_words, vs_scales, offs, offs2, offs3, offs4, offs5, offs6, offs7, out
):
    nc = tc.nc
    with ExitStack() as ctx:
        keep = ctx.enter_context(tc.tile_pool(name="keep", bufs=1))
        psum = ctx.enter_context(tc.psum_pool(name="psum", bufs=8))

        def list_tile(name, src):
            tile = keep.tile(list(src.shape), U16, name=name)
            nc.sync.dma_start(tile[:], src)
            return tile

        def steps_tile(name, src):
            tile = keep.tile([P, PACK], F32, name=name)
            nc.sync.dma_start(tile[:], src.rearrange("(p t) o -> p (t o)", t=PACK))
            return tile

        def table_tile(name, src, t):
            tile = keep.tile([P, src.shape[1]], F32, name=name)
            nc.sync.dma_start(tile[:], src.rearrange("(p t) c -> t p c", t=PACK)[t])
            return tile

        warm_in = keep.tile([P, 1], F32, name="warm_in")
        warm_out = keep.tile([P, 1], F32, name="warm_out")
        nc.vector.memset(warm_in[:], 0.0)
        nc.scalar.activation(warm_out[:], warm_in[:], ACT.Copy)
        ua_rows = [table_tile("ua0", ua, 0)]
        idx3 = list_tile("idx3", offs3)
        ha_t = steps_tile("ha_t", ha)
        ua_rows.extend(table_tile(f"ua{t}", ua, t) for t in range(1, PACK))
        idx1 = list_tile("idx1", offs)
        idx2 = list_tile("idx2", offs2)
        ga_t = steps_tile("ga_t", ga)
        gb_t = steps_tile("gb_t", gb)
        ta_rows = [table_tile(f"ta{t}", ta, t) for t in range(2)]
        idx7 = list_tile("idx7", offs7)
        vs_scale_table = keep.tile([P, S], U8, name="vs_scale_table")
        nc.vector.memset(vs_scale_table[:].bitcast(I32), 0)
        for q in range(4):
            nc.sync.dma_start(
                vs_scale_table[32 * q : 32 * q + 4, :].bitcast(I32), vs_scales[0, 4 * q : 4 * q + 4, :].bitcast(I32)
            )
        ta_rows.extend(table_tile(f"ta{t}", ta, t) for t in range(2, PACK))
        vs_word_table = keep.tile([P, S], U16, name="vs_word_table")
        nc.sync.dma_start(vs_word_table[:].bitcast(I32), vs_words[0].bitcast(I32))
        idx4 = list_tile("idx4", offs4)
        idx5 = list_tile("idx5", offs5)
        idx6 = list_tile("idx6", offs6)

        sa_t = steps_tile("sa_t", sa)
        sb_t = steps_tile("sb_t", sb)

        boards = [keep.tile([P, C], F32, name=f"board{t}") for t in range(PACK)]
        for board in boards:
            nc.vector.memset(board[:], 0.0)

        def fetch(dst, table, offsets, steps, t):
            nc.scalar.activation(dst, table[:].indirect(offsets), ACT.Copy, scale=steps[:, t : t + 1])

        wc_planes = keep.tile([P, PACK, R], BF16, name="wc_planes")
        for t in range(PACK):
            fetch(wc_planes[:, t, :], ua_rows[t], idx3[:], ha_t, t)
        wc_words = keep.tile([P, R * PACK], BF16, name="wc_words", align_bytes=64)
        nc.vector.tensor_copy(
            wc_words[:].rearrange("p (u m i t) -> p m t i u", u=PACK, i=2, t=PACK),
            wc_planes[:].rearrange("p t (m i u) -> p m t i u", i=2, u=PACK),
        )
        wc_codes = keep.tile([P, R], U32, name="wc_codes", align_bytes=64)
        wc_scales = keep.tile([P, R], U8, name="wc_scales", align_bytes=64)
        nc.vector.quantize_mx(wc_codes[:].bitcast(FP8X4), wc_scales[:], wc_words[:])

        vs_scale_picked = keep.tile([P, N], U8, name="vs_scale_picked", align_bytes=64)
        nc.vector.tensor_copy(vs_scale_picked[:], vs_scale_table[:].indirect(idx7[:]))
        vs_word_picked = keep.tile([P, N], U16, name="vs_word_picked", align_bytes=64)
        nc.vector.tensor_copy(vs_word_picked[:], vs_word_table[:].indirect(idx7[:]))

        def half_cols(h):
            return slice(h * HALF // STRIPE, (h + 1) * HALF // STRIPE)

        def product(u, codes, scales, slots):
            acc = psum.tile([P, slots.stop - slots.start], F32, name="acc")
            cols = slice(u * P, (u + 1) * P)
            nc.tensor.matmul_mx(
                acc[:], lhsT=wc_codes[:, cols].bitcast(FP8X4), lhsT_scale=wc_scales[:, cols],
                rhs=codes[:, slots].bitcast(FP8X4), rhs_scale=scales[:, slots], start=True, stop=True,
            )
            return acc

        def put(u, h, staged):
            nc.vector.tensor_copy(boards[u][:].indirect(idx4[:, half_cols(h)]), staged)

        def quantised(name, words, width):
            codes = keep.tile([P, width], U32, name=name + "_codes", align_bytes=64)
            scales = keep.tile([P, width], U8, name=name + "_scales", align_bytes=64)
            nc.vector.quantize_mx(codes[:].bitcast(FP8X4), scales[:], words[:].rearrange("p c t -> p (c t)"))
            return codes, scales

        terms = keep.tile([P, 2 * SLOTS * HALF], F32, name="terms")

        def term(side, h, t):
            start = (2 * (h + t) + side) * HALF
            return terms[:, start : start + HALF]

        def planes(side, h, ts, cols):
            slots = terms[:].rearrange("p (n s c) -> p s n c", s=2, n=SLOTS)
            return slots[:, side, h + ts.start : h + ts.stop, cols].rearrange("p t (c i) -> p c t i", i=4)

        def subtract(engine, words, h, ts, cols):
            engine.tensor_tensor(
                words[:, :, ts].rearrange("p (c i) t -> p c t i", i=4),
                planes(0, h, ts, cols), planes(1, h, ts, cols), ALU.subtract,
            )

        xc0 = [keep.tile([P, QUARTER, PACK], BF16, name=f"xc0_{q}", align_bytes=64) for q in range(2)]
        for t in range(PACK):
            fetch(term(0, 0, t), ta_rows[t], idx1[:, half_cols(0)], ga_t, t)
            fetch(term(1, 0, t), ta_rows[t], idx2[:, half_cols(0)], gb_t, t)
            if t % 2 == 1:
                for q in range(2):
                    subtract(nc.vector, xc0[q], 0, slice(t - 1, t + 1), slice(q * QUARTER, (q + 1) * QUARTER))
        x0_codes = keep.tile([P, HALF], U32, name="x0_codes", align_bytes=64)
        x0_scales = keep.tile([P, HALF], U8, name="x0_scales", align_bytes=64)
        for q in range(2):
            cols = slice(q * QUARTER, (q + 1) * QUARTER)
            nc.vector.quantize_mx(
                x0_codes[:, cols].bitcast(FP8X4), x0_scales[:, cols], xc0[q][:].rearrange("p c t -> p (c t)")
            )
        lead = [product(0, x0_codes, x0_scales, slice(q * QUARTER, (q + 1) * QUARTER)) for q in range(2)]
        acc0 = [product(u, x0_codes, x0_scales, slice(0, HALF)) for u in range(1, PACK)]
        for q in range(2):
            start = (2 * (1 + q) + 1) * HALF - QUARTER // 2
            staged = terms[:, start : start + QUARTER]
            nc.vector.tensor_copy(staged, lead[q][:])
            nc.vector.tensor_copy(
                boards[0][:].indirect(idx4[:, q * QUARTER // STRIPE : (q + 1) * QUARTER // STRIPE]), staged
            )
        for u in range(1, PACK - 1):
            staged = keep.tile([P, HALF], F32, name=f"staged0_{u}")
            nc.scalar.copy(staged[:], acc0[u - 1][:])
            put(u, 0, staged[:])

        for t in (3, 2, 0, 1):
            fetch(term(0, 1, t), ta_rows[t], idx1[:, half_cols(1)], ga_t, t)
            fetch(term(1, 1, t), ta_rows[t], idx2[:, half_cols(1)], gb_t, t)
        xc1 = keep.tile([P, HALF, PACK], BF16, name="xc1", align_bytes=64)
        for ts in (slice(2, 4), slice(0, 1), slice(1, 2)):
            subtract(nc.gpsimd, xc1, 1, ts, slice(0, HALF))
        x1_codes, x1_scales = quantised("xc1", xc1, HALF)
        staged_last = term(1, 1, 1)
        nc.scalar.copy(staged_last, acc0[PACK - 2][:])
        put(PACK - 1, 0, staged_last)

        first = keep.tile([P, PACK, O], F32, name="first")
        second = keep.tile([P, PACK, O], F32, name="second")
        staged1 = [keep.tile([P, HALF], F32, name=f"staged1_{u}") for u in range(PACK)]
        for u in range(PACK):
            nc.scalar.copy(staged1[u][:], product(u, x1_codes, x1_scales, slice(0, HALF))[:])
        for u in range(PACK):
            put(u, 1, staged1[u][:])
        for u in range(PACK):
            fetch(first[:, u, :], boards[u], idx5[:], sa_t, u)
            fetch(second[:, u, :], boards[u], idx6[:], sb_t, u)

        gap = keep.tile([P, PACK, O], BF16, name="gap")
        nc.vector.tensor_tensor(gap[:, : PACK - 1, :], first[:, : PACK - 1, :], second[:, : PACK - 1, :], ALU.subtract)
        nc.vector.tensor_tensor(gap[:, PACK - 1, :], first[:, PACK - 1, :], second[:, PACK - 1, :], ALU.subtract)
        hid_words = [keep.tile([P, PART, PACK], BF16, name=f"hid_words{part}", align_bytes=64) for part in range(2)]
        nc.scalar.activation(
            hid_words[0][:].rearrange("p (c i) t -> p c t i", i=4),
            gap[:, :, :PART].rearrange("p t (c i) -> p c t i", i=4),
            ACT.Abs,
        )
        gap_rest = gap[:, :, PART:].rearrange("p t c -> p c t")
        nc.vector.scalar_tensor_tensor(hid_words[1][:], gap_rest, -1.0, gap_rest, ALU.mult, ALU.max)
        results = [keep.tile([P, O], F32, name=f"result{b}") for b in range(2)]
        for part in range(2):
            codes, scales = quantised(f"hid{part}", hid_words[part], PART)
            for b, engine_copy in enumerate((nc.vector.tensor_copy, nc.scalar.copy)):
                rows = slice(b * P, (b + 1) * P)
                y = psum.tile([P, PART], F32, name="acc")
                nc.tensor.matmul_mx(
                    y[:], lhsT=vs_word_picked[:, rows].bitcast(FP4X4), lhsT_scale=vs_scale_picked[:, rows],
                    rhs=codes[:].bitcast(FP8X4), rhs_scale=scales[:], start=True, stop=True,
                )
                engine_copy(results[b][:, part * PART : (part + 1) * PART], y[:])
        for b, queue in enumerate((nc.sync, nc.scalar)):
            queue.dma_start(out[b * P : (b + 1) * P, :], results[b][:])
